import numpy as np
import ml_dtypes


def mxq(x, axis, fmt="e4m3"):
    dtype, down = {"e4m3": (ml_dtypes.float8_e4m3fn, 7), "e5m2": (ml_dtypes.float8_e5m2, 14)}[fmt]
    v = np.moveaxis(np.asarray(x, np.float32).astype(ml_dtypes.bfloat16).astype(np.float64), axis, -1)
    blocks = v.reshape(v.shape[:-1] + (-1, 32))
    amax = np.abs(blocks).max(-1, keepdims=True)
    byte = np.maximum(np.where(amax > 0, np.frexp(amax)[1] - 1 + 127, 0) - down, 1)
    scale = np.exp2(byte - 127.0)
    codes = (blocks / scale).astype(np.float32).astype(dtype).astype(np.float64)
    return np.moveaxis((codes * scale).reshape(v.shape), -1, axis)


WIDE = False


def mx_kscale(k):
    if not WIDE:
        return np.ones(k)
    levels = np.array([30, -30])
    if k % 512:
        return np.exp2(np.random.permutation(np.resize(levels, k // 32))).repeat(32)
    a = np.empty((k // 512, 16))
    for p in range(k // 512):
        a[p, :8] = np.random.permutation(np.resize(levels, 8))
        for g in range(8):
            far = levels[np.abs(levels - a[p, g]) >= 10]
            a[p, g + 8] = far[np.random.randint(len(far))]
    return np.exp2(a.ravel()).repeat(32)


BF16 = ml_dtypes.bfloat16


def bf(x):
    return np.asarray(x, np.float32).astype(BF16)


def f64(x):
    return np.asarray(x).astype(np.float64)


M, W, P, Q = 1024, 32, 64, 32


def setup_inputs():
    C, A = W * P, W * Q
    s, t = mx_kscale(C), mx_kscale(A)
    w = np.exp(0.3 * np.random.standard_normal(W))
    return {"phi_core": bf(np.random.standard_normal((M, C)) * s),
            "phi_act": bf(np.random.standard_normal((M, A)) * t),
            "inv_core": bf(1 + 0.3 * np.abs(np.random.standard_normal((W, P)))),
            "inv_act": bf(np.exp(0.8 * np.abs(np.random.standard_normal((W, Q))))),
            "weight": bf(w / w.mean()),
            "psi_core_t": bf(np.random.standard_normal((C, M)) / np.sqrt(C) / s[:, None]),
            "psi_act_t": bf(0.4 * np.random.standard_normal((A, M)) / np.sqrt(A) / t[:, None]),
            "frozen": bf(0.5 * np.random.standard_normal((M, M)))}


def reference(phi_core, phi_act, inv_core, inv_act, weight, psi_core_t, psi_act_t, frozen):
    w = f64(weight)[:, None]
    dc = (f64(inv_core) * w).reshape(-1)
    da = (f64(inv_act) * w).reshape(-1)
    tc = f64(phi_core) * dc
    ta = f64(phi_act) * da
    core = mxq(tc, 1, "e4m3") @ mxq(f64(psi_core_t), 0, "e4m3")
    act = mxq(ta, 1, "e5m2") @ mxq(f64(psi_act_t), 0, "e4m3")
    return core + act + f64(frozen)

@@ -1,0 +1,232 @@
+from contextlib import ExitStack
+
+import concourse.mybir as mybir
+from concourse.masks import make_identity
+
+M = 1024
+NB = 1024
+KC, KA = 2048, 1024
+FLOPS = 2 * M * NB * (KC + KA)
+
+F32 = mybir.dt.float32
+BF16 = mybir.dt.bfloat16
+U32 = mybir.dt.uint32
+U8 = mybir.dt.uint8
+E4 = mybir.dt.float8_e4m3fn_x4
+E5 = mybir.dt.float8_e5m2_x4
+ADD = mybir.AluOpType.add
+MULT = mybir.AluOpType.mult
+COPY = mybir.ActivationFunctionType.Copy
+
+P = 128
+PASSES = 6
+CORE = 4
+ORDER = (0, 1, 2, 3, 4, 5)
+HALF = 512
+
+STEPS = (
+    "I00 T00 T01 E00 E01 I01 P00 T02 Q00 Q01 T03 E02 M000 I02 M100 P01 Q02 M001 E03 M101 "
+    "T04 T05 E04 P02 Q03 M002 E05 M102 X04 T10 Q04 T11 I03 E10 X05 T12 Q10 Q05 T13 E11 "
+    "I04 M200 M300 P03 Q11 M003 E12 M103 M201 I05 M301 T14 P04 T15 Q12 E13 M004 M104 M202 M302 "
+    "E14 Q13 T20 P05 M203 E20 E15 M303 M005 M105 T21 X14 I10 T22 X15 T23 Q14 Q15 M204 Q20 "
+    "M304 E21 M205 I11 M305 M400 T24 E22 T25 Q21 Q22 M401 E23 E24 M402 T30 P10 E25 Q23 T31 "
+    "O00 M403 I12 O10 M500 M501 O20 M502 M503 O30 M010 M110 X24 M210 T32 P11 I13 Q24 M011 X25 "
+    "M404 M504 P12 M111 M211 Q25 M012 E30 M112 I14 M405 M505 M212 O40 T33 O50 M310 Q30 M410 M311 "
+    "P13 I15 M411 M312 E31 M412 M013 M113 M213 P14 M313 M413 Q31 M014 E32 M114 M214 M314 M414 P15 "
+    "T34 Q32 T35 E34 E33 M015 M115 O01 M215 E35 M315 O11 M510 M511 O21 M512 M600 O31 M700 M513 "
+    "Q33 M610 X34 M601 M701 M611 X35 M514 M602 Q34 M702 M612 Q35 M415 M515 O41 M603 M703 O51 M710 "
+    "M711 M712 M613 M713 M604 M704 M614 M714 M605 M705 O60 M615 M715 O70 O61 O71 "
+)
+
+
+def tile_afqmc_mixed_green_s2_kernel(
+    tc, phi_core, phi_act, inv_core, inv_act, weight, psi_core_t, psi_act_t, frozen, out
+):
+    nc = tc.nc
+    with ExitStack() as ctx:
+        keep = ctx.enter_context(tc.tile_pool(name="keep", bufs=1))
+        stage = ctx.enter_context(tc.tile_pool(name="stage", bufs=4))
+        outs = ctx.enter_context(tc.tile_pool(name="outs", bufs=6))
+        psum = ctx.enter_context(tc.psum_pool(name="psum", bufs=3))
+
+        inv = keep.tile([P, 512], BF16, name="inv")
+        wrow = keep.tile([P, 16], BF16, name="wrow")
+        nc.sync.dma_start(out=inv[0:4, :], in_=inv_core.rearrange("(g q) a -> g (q a)", g=4))
+        nc.sync.dma_start(out=wrow[0:4, 0:8], in_=weight.rearrange("(g q) -> g q", g=4))
+        nc.sync.dma_start(out=inv[32:34, :], in_=inv_act.rearrange("(g q) a -> g (q a)", g=2))
+        nc.sync.dma_start(out=wrow[32:34, 0:16], in_=weight.rearrange("(g q) -> g q", g=2))
+
+        phi = {}
+
+        def load_phi(pr, g0, n):
+            t = keep.tile([P, 2, 512 * n], BF16, name=f"phi_{pr}_{g0}")
+            src = phi_core if g0 < CORE else phi_act
+            k0 = 512 * (g0 if g0 < CORE else g0 - CORE)
+            nc.sync.dma_start(
+                out=t[:], in_=src[256 * pr : 256 * (pr + 1), k0 : k0 + 512 * n].rearrange("(t p) k -> p t k", p=P)
+            )
+            for i in range(n):
+                phi[(pr, g0 + i)] = (t, i)
+
+        raw = {}
+
+        def load_psi(h, g):
+            t = stage.tile([P, 4, HALF], BF16, name="praw", bufs=12)
+            src = psi_core_t if g < CORE else psi_act_t
+            k0 = 512 * (g if g < CORE else g - CORE)
+            nc.sync.dma_start(
+                out=t[:],
+                in_=src[k0 : k0 + 512, h * HALF : (h + 1) * HALF].rearrange("(p j) n -> p j n", j=4),
+            )
+            raw[(h, g)] = t
+
+        frz = keep.tile([P, 8, NB], BF16, name="frz")
+
+        def load_frz(i):
+            nc.sync.dma_start(
+                out=frz[:, 4 * i : 4 * i + 4, :], in_=frozen.rearrange("(t p) n -> p t n", p=P)[:, 4 * i : 4 * i + 4, :]
+            )
+
+        load_psi(0, 0)
+        load_phi(0, 0, 1)
+        load_phi(0, 1, 1)
+        load_psi(0, 1)
+        load_phi(0, 2, 2)
+        load_psi(0, 2)
+        load_phi(0, 4, 2)
+        load_psi(0, 3)
+        load_phi(1, 0, 2)
+        load_psi(0, 4)
+        load_phi(1, 2, 2)
+        load_psi(0, 5)
+        load_phi(1, 4, 2)
+        load_phi(2, 0, 4)
+        load_psi(1, 0)
+        load_phi(2, 4, 2)
+        load_psi(1, 1)
+        load_psi(1, 2)
+        load_phi(3, 0, 4)
+        load_frz(0)
+        load_psi(1, 3)
+        load_psi(1, 4)
+        load_frz(1)
+        load_psi(1, 5)
+        load_phi(3, 4, 2)
+
+        ident = keep.tile([P, P], F32, name="ident")
+        make_identity(nc, ident[:])
+        dnat = keep.tile([P, 512], F32, name="dnat")
+        nc.vector.memset(dnat[:], 0.0)
+        warm = keep.tile([P, 1], F32, name="warm")
+        nc.scalar.activation(warm[:], dnat[:, 0:1], COPY, scale=1.0)
+        nc.vector.tensor_tensor(
+            out=dnat[0:4, :].rearrange("g (q a) -> g q a", q=8),
+            in0=inv[0:4, :].rearrange("g (q a) -> g q a", q=8),
+            in1=wrow[0:4, 0:8].unsqueeze(2).to_broadcast([4, 8, 64]),
+            op=MULT,
+        )
+        nc.vector.tensor_tensor(
+            out=dnat[32:34, :].rearrange("g (q a) -> g q a", q=16),
+            in0=inv[32:34, :].rearrange("g (q a) -> g q a", q=16),
+            in1=wrow[32:34, 0:16].unsqueeze(2).to_broadcast([2, 16, 32]),
+            op=MULT,
+        )
+        dps = psum.tile([P, 4, P], F32, name="xt")
+        for j in range(4):
+            nc.tensor.transpose(dps[:, j, :], dnat[:, j:512:4], ident[:])
+        dT = keep.tile([P, PASSES, 4], F32, name="dT")
+        nc.vector.tensor_copy(out=dT[:, 0:4, :], in_=dps[:, :, 0:4].rearrange("p j g -> p g j"))
+        nc.vector.tensor_copy(out=dT[:, 4:6, :], in_=dps[:, :, 32:34].rearrange("p j g -> p g j"))
+
+        xc = [keep.tile([P, PASSES, 256], U32, align_bytes=64, name=f"xc{pr}") for pr in range(4)]
+        xs = [keep.tile([P, PASSES, 256], U8, align_bytes=64, name=f"xs{pr}") for pr in range(4)]
+        pc = [keep.tile([P, PASSES, HALF], U32, align_bytes=64, name=f"pc{h}") for h in range(2)]
+        ps = [keep.tile([P, PASSES, HALF], U8, align_bytes=64, name=f"ps{h}") for h in range(2)]
+
+        tiles = {}
+
+        def do_t(pr, g):
+            xt = psum.tile([P, 2, 256], F32, name="xt")
+            tiles[("xt", pr, g)] = xt
+            t, i = phi[(pr, g)]
+            words = t[:].bitcast(F32)
+            for r in range(2):
+                for u in range(2):
+                    src = words[:, r, 256 * i + u : 256 * (i + 1) : 2]
+                    nc.tensor.transpose(xt[:, u, r * P : (r + 1) * P], src, ident[:])
+
+        def do_e(pr, g):
+            xt = tiles[("xt", pr, g)]
+            gr = stage.tile([P, 256, 4], BF16, align_bytes=64, name="gr")
+            tiles[("gr", pr, g)] = gr
+            xb = xt[:].rearrange("p u r -> p (u r)").bitcast(BF16).rearrange("p (u r e) -> p r u e", u=2, e=2)
+            if g >= CORE:
+                pl = stage.tile([P, 4, 256], BF16, name="pl")
+                tiles[("pl", pr, g)] = pl
+                for j in range(4):
+                    nc.scalar.activation(pl[:, j, :], xb[:, :, j // 2, j % 2], COPY, scale=dT[:, g, j : j + 1])
+                return
+            nc.vector.tensor_tensor(
+                out=gr[:].rearrange("p r (u e) -> p r u e", u=2),
+                in0=xb,
+                in1=dT[:, g, :].rearrange("p (u e) -> p u e", u=2).unsqueeze(1).to_broadcast([P, 256, 2, 2]),
+                op=MULT,
+            )
+
+        def do_x(pr, g):
+            nc.vector.tensor_copy(
+                out=tiles[("gr", pr, g)][:].rearrange("p (c i) j -> p c j i", i=4),
+                in_=tiles[("pl", pr, g)][:].rearrange("p j (c i) -> p c j i", i=4),
+            )
+
+        def do_q(pr, g):
+            nc.vector.quantize_mx(
+                out=xc[pr][:, g, :].bitcast(E4 if g < CORE else E5),
+                scales=xs[pr][:, g, :],
+                in_=tiles[("gr", pr, g)][:].rearrange("p r j -> p (r j)"),
+            )
+
+        def do_i(h, g):
+            pg = stage.tile([P, HALF, 4], BF16, align_bytes=64, name="pg")
+            tiles[("pg", h, g)] = pg
+            nc.scalar.copy(
+                out=pg[:].rearrange("p (c i) j -> p c j i", i=4),
+                in_=raw[(h, g)][:].rearrange("p j (c i) -> p c j i", i=4),
+            )
+
+        def do_p(h, g):
+            nc.vector.quantize_mx(
+                out=pc[h][:, g, :].bitcast(E4),
+                scales=ps[h][:, g, :],
+                in_=tiles[("pg", h, g)][:].rearrange("p n j -> p (n j)"),
+            )
+
+        acc = {}
+
+        def do_m(rt, h, g):
+            if g == ORDER[0]:
+                a = psum.tile([P, HALF], F32, name="acc", bufs=5)
+                acc[(rt, h)] = a
+            fx = E4 if g < CORE else E5
+            cols = slice((rt % 2) * P, (rt % 2 + 1) * P)
+            nc.tensor.matmul_mx(
+                out=acc[(rt, h)][:],
+                lhsT=xc[rt // 2][:, g, cols].bitcast(fx),
+                lhsT_scale=xs[rt // 2][:, g, cols],
+                rhs=pc[h][:, g, :].bitcast(E4),
+                rhs_scale=ps[h][:, g, :],
+                start=(g == ORDER[0]),
+                stop=(g == ORDER[-1]),
+            )
+
+        def do_o(rt, h):
+            o = outs.tile([P, HALF], F32, name="o")
+            nc.vector.tensor_tensor(
+                out=o[:], in0=acc[(rt, h)][:], in1=frz[:, rt, h * HALF : (h + 1) * HALF], op=ADD
+            )
+            nc.sync.dma_start(out=out[rt * P : (rt + 1) * P, h * HALF : (h + 1) * HALF], in_=o[:])
+
+        steps = {"T": do_t, "E": do_e, "X": do_x, "Q": do_q, "I": do_i, "P": do_p, "M": do_m, "O": do_o}
+        ctx.enter_context(tc.manual_schedule())
+        for step in STEPS.split():
+            steps[step[0]](*[int(c) for c in step[1:]])

@@ -21,21 +21,24 @@ COPY = mybir.ActivationFunctionType.Copy
 P = 128
 PASSES = 6
 CORE = 4
-ORDER = (0, 1, 2, 3, 4, 5)
 HALF = 512
 
+ROWS_ON_VECTOR = ((1, 3),)
+ON_SCALAR = ((0, 1), (0, 3), (0, 4), (1, 1), (1, 2), (2, 4), (3, 1), (3, 3), (3, 4), (3, 5))
+
 STEPS = (
-    "I00 T00 T01 E00 E01 I01 P00 T02 Q00 Q01 T03 E02 M000 I02 M100 P01 Q02 M001 E03 M101 "
-    "T04 T05 E04 P02 Q03 M002 E05 M102 X04 T10 Q04 T11 I03 E10 X05 T12 Q10 Q05 T13 E11 "
-    "I04 M200 M300 P03 Q11 M003 E12 M103 M201 I05 M301 T14 P04 T15 Q12 E13 M004 M104 M202 M302 "
-    "E14 Q13 T20 P05 M203 E20 E15 M303 M005 M105 T21 X14 I10 T22 X15 T23 Q14 Q15 M204 Q20 "
-    "M304 E21 M205 I11 M305 M400 T24 E22 T25 Q21 Q22 M401 E23 E24 M402 T30 P10 E25 Q23 T31 "
-    "O00 M403 I12 O10 M500 M501 O20 M502 M503 O30 M010 M110 X24 M210 T32 P11 I13 Q24 M011 X25 "
-    "M404 M504 P12 M111 M211 Q25 M012 E30 M112 I14 M405 M505 M212 O40 T33 O50 M310 Q30 M410 M311 "
-    "P13 I15 M411 M312 E31 M412 M013 M113 M213 P14 M313 M413 Q31 M014 E32 M114 M214 M314 M414 P15 "
-    "T34 Q32 T35 E34 E33 M015 M115 O01 M215 E35 M315 O11 M510 M511 O21 M512 M600 O31 M700 M513 "
-    "Q33 M610 X34 M601 M701 M611 X35 M514 M602 Q34 M702 M612 Q35 M415 M515 O41 M603 M703 O51 M710 "
-    "M711 M712 M613 M713 M604 M704 M614 M714 M605 M705 O60 M615 M715 O70 O61 O71 "
+    "T00 T11 E00 E11 Q00 T10 E10 X11 Q10 T02 Q11 T03 E02 I01 P01 Q02 T01 E03 E01 T14 T04 E14 "
+    "X03 T05 E04 X01 Q03 M301 T15 I04 Q01 E05 T13 T12 Q14 X04 E15 Q05 E13 I05 Q04 E12 P04 "
+    "T21 Q15 M001 Q13 T23 P05 I03 E21 I02 M004 M101 E23 M201 M205 T22 E22 M204 Q21 P03 X12 "
+    "Q22 M005 M304 T20 T24 I00 T25 Q12 P02 M401 M103 M104 M305 M203 Q23 E25 P00 M303 E24 "
+    "M003 Q25 M402 M102 M403 M202 M302 E20 M105 I10 X24 M002 M200 M100 Q20 Q24 M000 M300 "
+    "M405 T31 O30 T30 O10 O00 I12 T32 M400 M505 P10 M500 E31 M503 M504 M404 O20 M502 P12 "
+    "M010 J13 O40 M210 M501 M012 I14 M212 O50 M410 P13 T33 M412 M312 P14 M310 M112 I15 M110 "
+    "M013 M113 E32 M313 M114 P15 M314 I11 E30 M413 M213 M014 Q32 M414 X31 M214 M015 P11 E33 "
+    "M415 M315 M215 T35 T34 Q30 M115 M011 M311 M211 Q31 M111 M411 O01 O21 E34 M515 M513 M611 "
+    "M511 O41 M712 O31 X34 O11 M710 M610 M514 M512 M701 M601 X33 Q34 M510 Q33 M612 M600 M614 "
+    "E35 X35 M704 M702 M700 Q35 M603 M703 M705 M615 M602 O51 M714 O70 M613 M604 M605 M713 "
+    "O61 M715 M711 O60 O71 "
 )
 
 
@@ -71,14 +74,22 @@ def tile_afqmc_mixed_green_s2_kernel(
         raw = {}
 
         def load_psi(h, g):
-            t = stage.tile([P, 4, HALF], BF16, name="praw", bufs=12)
+            t = stage.tile([P, 4, HALF], BF16, name="praw", bufs=8)
             src = psi_core_t if g < CORE else psi_act_t
             k0 = 512 * (g if g < CORE else g - CORE)
             nc.sync.dma_start(
                 out=t[:],
                 in_=src[k0 : k0 + 512, h * HALF : (h + 1) * HALF].rearrange("(p j) n -> p j n", j=4),
             )
-            raw[(h, g)] = t
+            raw[(h, g)] = t[:]
+
+        def load_psi_row(g):
+            t = stage.tile([P, 4, NB], BF16, name="prow", bufs=2)
+            src = psi_core_t if g < CORE else psi_act_t
+            k0 = 512 * (g if g < CORE else g - CORE)
+            nc.sync.dma_start(out=t[:], in_=src[k0 : k0 + 512, :].rearrange("(p j) n -> p j n", j=4))
+            for h in range(2):
+                raw[(h, g)] = t[:, :, h * HALF : (h + 1) * HALF]
 
         frz = keep.tile([P, 8, NB], BF16, name="frz")
 
@@ -87,30 +98,29 @@ def tile_afqmc_mixed_green_s2_kernel(
                 out=frz[:, 4 * i : 4 * i + 4, :], in_=frozen.rearrange("(t p) n -> p t n", p=P)[:, 4 * i : 4 * i + 4, :]
             )
 
-        load_psi(0, 0)
         load_phi(0, 0, 1)
-        load_phi(0, 1, 1)
+        load_phi(1, 0, 2)
         load_psi(0, 1)
         load_phi(0, 2, 2)
-        load_psi(0, 2)
+        load_phi(0, 1, 1)
+        load_phi(1, 4, 2)
         load_phi(0, 4, 2)
-        load_psi(0, 3)
-        load_phi(1, 0, 2)
         load_psi(0, 4)
         load_phi(1, 2, 2)
         load_psi(0, 5)
-        load_phi(1, 4, 2)
         load_phi(2, 0, 4)
-        load_psi(1, 0)
+        load_psi(0, 3)
+        load_psi_row(2)
         load_phi(2, 4, 2)
-        load_psi(1, 1)
-        load_psi(1, 2)
-        load_phi(3, 0, 4)
+        load_psi_row(0)
         load_frz(0)
         load_psi(1, 3)
+        load_phi(3, 0, 2)
+        load_phi(3, 2, 2)
         load_psi(1, 4)
         load_frz(1)
         load_psi(1, 5)
+        load_psi(1, 1)
         load_phi(3, 4, 2)
 
         ident = keep.tile([P, P], F32, name="ident")
@@ -160,7 +170,7 @@ def tile_afqmc_mixed_green_s2_kernel(
             gr = stage.tile([P, 256, 4], BF16, align_bytes=64, name="gr")
             tiles[("gr", pr, g)] = gr
             xb = xt[:].rearrange("p u r -> p (u r)").bitcast(BF16).rearrange("p (u r e) -> p r u e", u=2, e=2)
-            if g >= CORE:
+            if (pr, g) in ON_SCALAR:
                 pl = stage.tile([P, 4, 256], BF16, name="pl")
                 tiles[("pl", pr, g)] = pl
                 for j in range(4):
@@ -189,9 +199,9 @@ def tile_afqmc_mixed_green_s2_kernel(
         def do_i(h, g):
             pg = stage.tile([P, HALF, 4], BF16, align_bytes=64, name="pg")
             tiles[("pg", h, g)] = pg
-            nc.scalar.copy(
+            (nc.vector.tensor_copy if (h, g) in ROWS_ON_VECTOR else nc.scalar.copy)(
                 out=pg[:].rearrange("p (c i) j -> p c j i", i=4),
-                in_=raw[(h, g)][:].rearrange("p j (c i) -> p c j i", i=4),
+                in_=raw[(h, g)].rearrange("p j (c i) -> p c j i", i=4),
             )
 
         def do_p(h, g):
@@ -202,9 +212,12 @@ def tile_afqmc_mixed_green_s2_kernel(
             )
 
         acc = {}
+        left = {}
 
         def do_m(rt, h, g):
-            if g == ORDER[0]:
+            first = (rt, h) not in acc
+            left[(rt, h)] = left.get((rt, h), PASSES) - 1
+            if first:
                 a = psum.tile([P, HALF], F32, name="acc", bufs=5)
                 acc[(rt, h)] = a
             fx = E4 if g < CORE else E5
@@ -215,8 +228,8 @@ def tile_afqmc_mixed_green_s2_kernel(
                 lhsT_scale=xs[rt // 2][:, g, cols],
                 rhs=pc[h][:, g, :].bitcast(E4),
                 rhs_scale=ps[h][:, g, :],
-                start=(g == ORDER[0]),
-                stop=(g == ORDER[-1]),
+                start=first,
+                stop=(left[(rt, h)] == 0),
             )
 
         def do_o(rt, h):
@@ -226,7 +239,7 @@ def tile_afqmc_mixed_green_s2_kernel(
             )
             nc.sync.dma_start(out=out[rt * P : (rt + 1) * P, h * HALF : (h + 1) * HALF], in_=o[:])
 
-        steps = {"T": do_t, "E": do_e, "X": do_x, "Q": do_q, "I": do_i, "P": do_p, "M": do_m, "O": do_o}
+        steps = {"T": do_t, "E": do_e, "X": do_x, "Q": do_q, "I": do_i, "J": do_i, "P": do_p, "M": do_m, "O": do_o}
         ctx.enter_context(tc.manual_schedule())
         for step in STEPS.split():
             steps[step[0]](*[int(c) for c in step[1:]])

from contextlib import ExitStack

import concourse.mybir as mybir
from concourse.masks import make_identity

M = 1024
NB = 1024
KC, KA = 2048, 1024
FLOPS = 2 * M * NB * (KC + KA)

F32 = mybir.dt.float32
BF16 = mybir.dt.bfloat16
U32 = mybir.dt.uint32
U8 = mybir.dt.uint8
E4 = mybir.dt.float8_e4m3fn_x4
E5 = mybir.dt.float8_e5m2_x4
ADD = mybir.AluOpType.add
MULT = mybir.AluOpType.mult
COPY = mybir.ActivationFunctionType.Copy

P = 128
PASSES = 6
CORE = 4
HALF = 512

ROWS_ON_VECTOR = ((1, 3),)
ON_SCALAR = ((0, 1), (0, 3), (0, 4), (1, 1), (1, 2), (2, 4), (3, 1), (3, 3), (3, 4), (3, 5))

STEPS = (
    "T00 T11 E00 E11 Q00 T10 E10 X11 Q10 T02 Q11 T03 E02 I01 P01 Q02 T01 E03 E01 T14 T04 E14 "
    "X03 T05 E04 X01 Q03 M301 T15 I04 Q01 E05 T13 T12 Q14 X04 E15 Q05 E13 I05 Q04 E12 P04 "
    "T21 Q15 M001 Q13 T23 P05 I03 E21 I02 M004 M101 E23 M201 M205 T22 E22 M204 Q21 P03 X12 "
    "Q22 M005 M304 T20 T24 I00 T25 Q12 P02 M401 M103 M104 M305 M203 Q23 E25 P00 M303 E24 "
    "M003 Q25 M402 M102 M403 M202 M302 E20 M105 I10 X24 M002 M200 M100 Q20 Q24 M000 M300 "
    "M405 T31 O30 T30 O10 O00 I12 T32 M400 M505 P10 M500 E31 M503 M504 M404 O20 M502 P12 "
    "M010 J13 O40 M210 M501 M012 I14 M212 O50 M410 P13 T33 M412 M312 P14 M310 M112 I15 M110 "
    "M013 M113 E32 M313 M114 P15 M314 I11 E30 M413 M213 M014 Q32 M414 X31 M214 M015 P11 E33 "
    "M415 M315 M215 T35 T34 Q30 M115 M011 M311 M211 Q31 M111 M411 O01 O21 E34 M515 M513 M611 "
    "M511 O41 M712 O31 X34 O11 M710 M610 M514 M512 M701 M601 X33 Q34 M510 Q33 M612 M600 M614 "
    "E35 X35 M704 M702 M700 Q35 M603 M703 M705 M615 M602 O51 M714 O70 M613 M604 M605 M713 "
    "O61 M715 M711 O60 O71 "
)


def tile_afqmc_mixed_green_s2_kernel(
    tc, phi_core, phi_act, inv_core, inv_act, weight, psi_core_t, psi_act_t, frozen, out
):
    nc = tc.nc
    with ExitStack() as ctx:
        keep = ctx.enter_context(tc.tile_pool(name="keep", bufs=1))
        stage = ctx.enter_context(tc.tile_pool(name="stage", bufs=4))
        outs = ctx.enter_context(tc.tile_pool(name="outs", bufs=6))
        psum = ctx.enter_context(tc.psum_pool(name="psum", bufs=3))

        inv = keep.tile([P, 512], BF16, name="inv")
        wrow = keep.tile([P, 16], BF16, name="wrow")
        nc.sync.dma_start(out=inv[0:4, :], in_=inv_core.rearrange("(g q) a -> g (q a)", g=4))
        nc.sync.dma_start(out=wrow[0:4, 0:8], in_=weight.rearrange("(g q) -> g q", g=4))
        nc.sync.dma_start(out=inv[32:34, :], in_=inv_act.rearrange("(g q) a -> g (q a)", g=2))
        nc.sync.dma_start(out=wrow[32:34, 0:16], in_=weight.rearrange("(g q) -> g q", g=2))

        phi = {}

        def load_phi(pr, g0, n):
            t = keep.tile([P, 2, 512 * n], BF16, name=f"phi_{pr}_{g0}")
            src = phi_core if g0 < CORE else phi_act
            k0 = 512 * (g0 if g0 < CORE else g0 - CORE)
            nc.sync.dma_start(
                out=t[:], in_=src[256 * pr : 256 * (pr + 1), k0 : k0 + 512 * n].rearrange("(t p) k -> p t k", p=P)
            )
            for i in range(n):
                phi[(pr, g0 + i)] = (t, i)

        raw = {}

        def load_psi(h, g):
            t = stage.tile([P, 4, HALF], BF16, name="praw", bufs=8)
            src = psi_core_t if g < CORE else psi_act_t
            k0 = 512 * (g if g < CORE else g - CORE)
            nc.sync.dma_start(
                out=t[:],
                in_=src[k0 : k0 + 512, h * HALF : (h + 1) * HALF].rearrange("(p j) n -> p j n", j=4),
            )
            raw[(h, g)] = t[:]

        def load_psi_row(g):
            t = stage.tile([P, 4, NB], BF16, name="prow", bufs=2)
            src = psi_core_t if g < CORE else psi_act_t
            k0 = 512 * (g if g < CORE else g - CORE)
            nc.sync.dma_start(out=t[:], in_=src[k0 : k0 + 512, :].rearrange("(p j) n -> p j n", j=4))
            for h in range(2):
                raw[(h, g)] = t[:, :, h * HALF : (h + 1) * HALF]

        frz = keep.tile([P, 8, NB], BF16, name="frz")

        def load_frz(i):
            nc.sync.dma_start(
                out=frz[:, 4 * i : 4 * i + 4, :], in_=frozen.rearrange("(t p) n -> p t n", p=P)[:, 4 * i : 4 * i + 4, :]
            )

        load_phi(0, 0, 1)
        load_phi(1, 0, 2)
        load_psi(0, 1)
        load_phi(0, 2, 2)
        load_phi(0, 1, 1)
        load_phi(1, 4, 2)
        load_phi(0, 4, 2)
        load_psi(0, 4)
        load_phi(1, 2, 2)
        load_psi(0, 5)
        load_phi(2, 0, 4)
        load_psi(0, 3)
        load_psi_row(2)
        load_phi(2, 4, 2)
        load_psi_row(0)
        load_frz(0)
        load_psi(1, 3)
        load_phi(3, 0, 2)
        load_phi(3, 2, 2)
        load_psi(1, 4)
        load_frz(1)
        load_psi(1, 5)
        load_psi(1, 1)
        load_phi(3, 4, 2)

        ident = keep.tile([P, P], F32, name="ident")
        make_identity(nc, ident[:])
        dnat = keep.tile([P, 512], F32, name="dnat")
        nc.vector.memset(dnat[:], 0.0)
        warm = keep.tile([P, 1], F32, name="warm")
        nc.scalar.activation(warm[:], dnat[:, 0:1], COPY, scale=1.0)
        nc.vector.tensor_tensor(
            out=dnat[0:4, :].rearrange("g (q a) -> g q a", q=8),
            in0=inv[0:4, :].rearrange("g (q a) -> g q a", q=8),
            in1=wrow[0:4, 0:8].unsqueeze(2).to_broadcast([4, 8, 64]),
            op=MULT,
        )
        nc.vector.tensor_tensor(
            out=dnat[32:34, :].rearrange("g (q a) -> g q a", q=16),
            in0=inv[32:34, :].rearrange("g (q a) -> g q a", q=16),
            in1=wrow[32:34, 0:16].unsqueeze(2).to_broadcast([2, 16, 32]),
            op=MULT,
        )
        dps = psum.tile([P, 4, P], F32, name="xt")
        for j in range(4):
            nc.tensor.transpose(dps[:, j, :], dnat[:, j:512:4], ident[:])
        dT = keep.tile([P, PASSES, 4], F32, name="dT")
        nc.vector.tensor_copy(out=dT[:, 0:4, :], in_=dps[:, :, 0:4].rearrange("p j g -> p g j"))
        nc.vector.tensor_copy(out=dT[:, 4:6, :], in_=dps[:, :, 32:34].rearrange("p j g -> p g j"))

        xc = [keep.tile([P, PASSES, 256], U32, align_bytes=64, name=f"xc{pr}") for pr in range(4)]
        xs = [keep.tile([P, PASSES, 256], U8, align_bytes=64, name=f"xs{pr}") for pr in range(4)]
        pc = [keep.tile([P, PASSES, HALF], U32, align_bytes=64, name=f"pc{h}") for h in range(2)]
        ps = [keep.tile([P, PASSES, HALF], U8, align_bytes=64, name=f"ps{h}") for h in range(2)]

        tiles = {}

        def do_t(pr, g):
            xt = psum.tile([P, 2, 256], F32, name="xt")
            tiles[("xt", pr, g)] = xt
            t, i = phi[(pr, g)]
            words = t[:].bitcast(F32)
            for r in range(2):
                for u in range(2):
                    src = words[:, r, 256 * i + u : 256 * (i + 1) : 2]
                    nc.tensor.transpose(xt[:, u, r * P : (r + 1) * P], src, ident[:])

        def do_e(pr, g):
            xt = tiles[("xt", pr, g)]
            gr = stage.tile([P, 256, 4], BF16, align_bytes=64, name="gr")
            tiles[("gr", pr, g)] = gr
            xb = xt[:].rearrange("p u r -> p (u r)").bitcast(BF16).rearrange("p (u r e) -> p r u e", u=2, e=2)
            if (pr, g) in ON_SCALAR:
                pl = stage.tile([P, 4, 256], BF16, name="pl")
                tiles[("pl", pr, g)] = pl
                for j in range(4):
                    nc.scalar.activation(pl[:, j, :], xb[:, :, j // 2, j % 2], COPY, scale=dT[:, g, j : j + 1])
                return
            nc.vector.tensor_tensor(
                out=gr[:].rearrange("p r (u e) -> p r u e", u=2),
                in0=xb,
                in1=dT[:, g, :].rearrange("p (u e) -> p u e", u=2).unsqueeze(1).to_broadcast([P, 256, 2, 2]),
                op=MULT,
            )

        def do_x(pr, g):
            nc.vector.tensor_copy(
                out=tiles[("gr", pr, g)][:].rearrange("p (c i) j -> p c j i", i=4),
                in_=tiles[("pl", pr, g)][:].rearrange("p j (c i) -> p c j i", i=4),
            )

        def do_q(pr, g):
            nc.vector.quantize_mx(
                out=xc[pr][:, g, :].bitcast(E4 if g < CORE else E5),
                scales=xs[pr][:, g, :],
                in_=tiles[("gr", pr, g)][:].rearrange("p r j -> p (r j)"),
            )

        def do_i(h, g):
            pg = stage.tile([P, HALF, 4], BF16, align_bytes=64, name="pg")
            tiles[("pg", h, g)] = pg
            (nc.vector.tensor_copy if (h, g) in ROWS_ON_VECTOR else nc.scalar.copy)(
                out=pg[:].rearrange("p (c i) j -> p c j i", i=4),
                in_=raw[(h, g)].rearrange("p j (c i) -> p c j i", i=4),
            )

        def do_p(h, g):
            nc.vector.quantize_mx(
                out=pc[h][:, g, :].bitcast(E4),
                scales=ps[h][:, g, :],
                in_=tiles[("pg", h, g)][:].rearrange("p n j -> p (n j)"),
            )

        acc = {}
        left = {}

        def do_m(rt, h, g):
            first = (rt, h) not in acc
            left[(rt, h)] = left.get((rt, h), PASSES) - 1
            if first:
                a = psum.tile([P, HALF], F32, name="acc", bufs=5)
                acc[(rt, h)] = a
            fx = E4 if g < CORE else E5
            cols = slice((rt % 2) * P, (rt % 2 + 1) * P)
            nc.tensor.matmul_mx(
                out=acc[(rt, h)][:],
                lhsT=xc[rt // 2][:, g, cols].bitcast(fx),
                lhsT_scale=xs[rt // 2][:, g, cols],
                rhs=pc[h][:, g, :].bitcast(E4),
                rhs_scale=ps[h][:, g, :],
                start=first,
                stop=(left[(rt, h)] == 0),
            )

        def do_o(rt, h):
            o = outs.tile([P, HALF], F32, name="o")
            nc.vector.tensor_tensor(
                out=o[:], in0=acc[(rt, h)][:], in1=frz[:, rt, h * HALF : (h + 1) * HALF], op=ADD
            )
            nc.sync.dma_start(out=out[rt * P : (rt + 1) * P, h * HALF : (h + 1) * HALF], in_=o[:])

        steps = {"T": do_t, "E": do_e, "X": do_x, "Q": do_q, "I": do_i, "J": do_i, "P": do_p, "M": do_m, "O": do_o}
        ctx.enter_context(tc.manual_schedule())
        for step in STEPS.split():
            steps[step[0]](*[int(c) for c in step[1:]])
